import numpy as np
import ml_dtypes


def mxq(x, axis, fmt="e4m3"):
    dtype, down = {"e4m3": (ml_dtypes.float8_e4m3fn, 7), "e5m2": (ml_dtypes.float8_e5m2, 14)}[fmt]
    v = np.moveaxis(np.asarray(x, np.float32).astype(ml_dtypes.bfloat16).astype(np.float64), axis, -1)
    blocks = v.reshape(v.shape[:-1] + (-1, 32))
    amax = np.abs(blocks).max(-1, keepdims=True)
    byte = np.maximum(np.where(amax > 0, np.frexp(amax)[1] - 1 + 127, 0) - down, 1)
    scale = np.exp2(byte - 127.0)
    codes = (blocks / scale).astype(np.float32).astype(dtype).astype(np.float64)
    return np.moveaxis((codes * scale).reshape(v.shape), -1, axis)


WIDE = False


def mx_kscale(k):
    if not WIDE:
        return np.ones(k)
    levels = np.array([10, -10, 5, -5, 0])
    if k % 512:
        return np.exp2(np.random.permutation(np.resize(levels, k // 32))).repeat(32)
    a = np.empty((k // 512, 16))
    for p in range(k // 512):
        a[p, :8] = np.random.permutation(np.resize(levels, 8))
        for g in range(8):
            far = levels[np.abs(levels - a[p, g]) >= 10]
            a[p, g + 8] = far[np.random.randint(len(far))]
    return np.exp2(a.ravel()).repeat(32)


BF16 = ml_dtypes.bfloat16


def bf(x):
    return np.asarray(x, np.float32).astype(BF16)


def f64(x):
    return np.asarray(x).astype(np.float64)


E2M1 = np.array([0.0, 0.5, 1.0, 1.5, 2.0, 3.0, 4.0, 6.0, -0.0, -0.5, -1.0, -1.5, -2.0, -3.0, -4.0, -6.0])


def pack_weight(w, fmt):
    k, n = w.shape
    w = f64(bf(w)).reshape(k // 32, 32, n)
    amax = np.abs(w).max(1)
    if fmt == "e4m3":
        byte = np.frexp(amax)[1] - 1 + 127 - 7
    else:
        mant, ex = np.frexp(amax / 6.0)
        byte = np.where(mant > 0.5, ex, ex - 1) + 127
    byte = np.clip(np.where(amax > 0, byte, 1), 1, 254)
    scaled = (w * np.exp2(127.0 - byte)[:, None, :]).reshape(k, n).astype(np.float32)
    by_word = np.ascontiguousarray(scaled.reshape(k // 512, 128, 4, n).transpose(0, 1, 3, 2))
    if fmt == "e4m3":
        words = by_word.astype(ml_dtypes.float8_e4m3fn).view(np.uint8)
    else:
        c = by_word.astype(ml_dtypes.float4_e2m1fn).view(np.uint8) & 0xF
        words = c[..., 0::2] | (c[..., 1::2] << 4)
    return np.ascontiguousarray(words), np.ascontiguousarray(byte.astype(np.uint8).reshape(k // 512, 16, n))


def unpack_weight(words, scales, fmt):
    g, p, n, _ = words.shape
    if fmt == "e4m3":
        vals = np.ascontiguousarray(words).view(ml_dtypes.float8_e4m3fn).astype(np.float64)
    else:
        nib = np.empty((g, p, n, 4), np.uint8)
        nib[..., 0::2] = words & 0xF
        nib[..., 1::2] = words >> 4
        vals = E2M1[nib]
    vals = vals * np.repeat(np.exp2(scales.astype(np.float64) - 127.0), 8, axis=1)[..., None]
    return vals.transpose(0, 1, 3, 2).reshape(g * 512, n)
def pack4(w):
    words, scales = pack_weight(w, "e2m1")
    return words.reshape(words.shape[0], 128, -1), scales


def unpack4(words, scales):
    return unpack_weight(words.reshape(words.shape[0], 128, -1, 2), scales, "e2m1")


M, K, F, T, D = 2048, 1024, 512, 2048, 1024


def setup_inputs():
    s, v, u = mx_kscale(K), mx_kscale(M), mx_kscale(D)
    radar = np.random.standard_normal((K, M)) * s[:, None]
    enc = np.random.standard_normal((K, F)) / np.sqrt(K) / s[:, None]
    align = np.random.standard_normal((M, T)) / np.sqrt(M) / v[:, None]
    radar_words, radar_scales = pack4(radar)
    enc_words, enc_scales = pack4(enc)
    align_words, align_scales = pack_weight(align, "e4m3")
    return {"radar_words": radar_words, "radar_scales": radar_scales,
            "enc_words": enc_words, "enc_scales": enc_scales,
            "trust": bf((0.5 + np.random.random(M)) * v),
            "align_words": align_words, "align_scales": align_scales,
            "camera": bf(np.random.standard_normal((T, D)) * u),
            "w_cam": bf(np.random.standard_normal((D, F)) / np.sqrt(D) / u[:, None]),
            "bias": bf(0.3 * np.random.standard_normal(F))}


def reference(radar_words, radar_scales, enc_words, enc_scales, trust, align_words, align_scales, camera, w_cam, bias):
    radar = unpack4(radar_words, radar_scales)
    enc = unpack4(enc_words, enc_scales)
    align = unpack_weight(align_words, align_scales, "e4m3")
    h = np.maximum(radar.T @ enc, 0.0) * f64(trust)[:, None]
    moved = align.T @ mxq(h, 0, "e4m3")
    seen = mxq(f64(camera), 1, "e4m3") @ mxq(f64(w_cam), 0, "e4m3")
    return moved + seen + f64(bias)

@@ -1,0 +1,352 @@
+from contextlib import ExitStack
+
+import concourse.mybir as mybir
+from concourse.masks import make_identity
+
+M, K, F, T, D = 2048, 1024, 512, 2048, 1024
+FLOPS = 2 * (K * M * F + M * T * F + T * D * F)
+
+F32 = mybir.dt.float32
+BF16 = mybir.dt.bfloat16
+I32 = mybir.dt.int32
+U32 = mybir.dt.uint32
+U16 = mybir.dt.uint16
+U8 = mybir.dt.uint8
+FP8X4 = mybir.dt.float8_e4m3fn_x4
+FP4X4 = mybir.dt.float4_e2m1fn_x4
+ALU = mybir.AluOpType
+
+P = 128
+PACK = 4
+PASS = P * PACK
+KP = K // PASS
+MP = M // PASS
+DP = D // PASS
+TILES = T // P
+QUARTERS = F // P
+CHUNK = 512
+EARLY = 4
+
+
+def tile_radar_camera_fusion_s4_kernel(
+    tc, radar_words, radar_scales, enc_words, enc_scales, trust, align_words, align_scales, camera, w_cam, bias, out
+):
+    nc = tc.nc
+    with ExitStack() as ctx:
+        keep = ctx.enter_context(tc.tile_pool(name="keep", bufs=1))
+        stream = ctx.enter_context(tc.tile_pool(name="stream", bufs=4))
+        psum = ctx.enter_context(tc.psum_pool(name="psum", bufs=1))
+        ctx.enter_context(tc.manual_schedule())
+
+        def kept(name, shape, dtype):
+            return keep.tile(shape, dtype, name=name, align_bytes=64)
+
+        def streamed(name, shape, dtype, bufs=4):
+            return stream.tile(shape, dtype, name=name, bufs=bufs, align_bytes=64)
+
+        def bank(index):
+            return psum.tile([P, F], F32, name="bank%d" % index)
+
+        work_count = []
+
+        def work_bank():
+            work_count.append(0)
+            return bank((len(work_count) - 1) % 4)
+
+        r_raw = [kept("r_raw%d" % g, [P, KP, 2 * PASS], U8) for g in range(MP)]
+        rs_first = kept("rs_first", [P, KP, PASS], U8)
+        rs_rest = kept("rs_rest", [P, KP, M - PASS], U8)
+        e_codes = kept("e_codes", [P, KP, 2 * F], U8)
+        e_scales = kept("e_scales", [P, KP, F], U8)
+        a_codes = [kept("a_codes%d" % c, [P, MP, CHUNK], U32) for c in range(T // CHUNK)]
+        a_scales = kept("a_scales", [P, T], U8)
+        cam_raw = [kept("cam_raw%d" % c, [P, 2, D], BF16) for c in range(TILES // 2)]
+        w_raw = [kept("w_raw%d" % k, [P, PACK, F], BF16) for k in range(DP)]
+        trust_sb = kept("trust_sb", [P, MP, PACK], BF16)
+        bias_col = kept("bias_col", [P, PACK], BF16)
+        ident = kept("ident", [P, P], F32)
+
+        nc.vector.memset(rs_first[:].rearrange("p k n -> p (k n)").bitcast(I32), 0)
+        nc.vector.memset(e_scales[:].rearrange("p k n -> p (k n)").bitcast(I32), 0)
+        nc.vector.memset(rs_rest[:].rearrange("p k n -> p (k n)").bitcast(I32), 0)
+        nc.vector.memset(a_scales[:].bitcast(I32), 0)
+        nc.gpsimd.dma_start(out=trust_sb[:], in_=trust.rearrange("(g p t) -> p g t", p=P, t=PACK))
+        make_identity(nc, ident[:])
+        nc.gpsimd.dma_start(out=bias_col[:], in_=bias.rearrange("(p t) -> p t", t=PACK))
+
+        def load_radar(g):
+            src = radar_words[:, :, 2 * PASS * g : 2 * PASS * (g + 1)].rearrange("k p n -> p k n")
+            nc.sync.dma_start(out=r_raw[g][:].bitcast(I32), in_=src.bitcast(I32))
+
+        def load_scale_rows(plane, rows):
+            for q in range(4):
+                src = rows[:, 4 * q : 4 * q + 4, :].rearrange("k r n -> r k n")
+                nc.sync.dma_start(out=plane[32 * q : 32 * q + 4, :, :].bitcast(I32), in_=src.bitcast(I32))
+
+        def load_align_scales():
+            for q in range(4):
+                src = align_scales[:, 4 * q : 4 * q + 4, :]
+                nc.sync.dma_start(out=a_scales[32 * q : 32 * q + 16, :].bitcast(I32), in_=src.bitcast(I32))
+
+        def load_align(c):
+            src = align_words[:, :, CHUNK * c : CHUNK * (c + 1), :].rearrange("g p n t -> p g (n t)")
+            nc.sync.dma_start(out=a_codes[c][:].bitcast(I32), in_=src.bitcast(I32))
+
+        def load_camera(c):
+            src = camera[2 * P * c : 2 * P * (c + 1), :].rearrange("(j p) d -> p j d", p=P)
+            nc.sync.dma_start(out=cam_raw[c][:], in_=src)
+
+        def load_w(k):
+            src = w_cam[PASS * k : PASS * (k + 1), :].rearrange("(p j) f -> p j f", j=PACK)
+            nc.sync.dma_start(out=w_raw[k][:], in_=src)
+
+        load_radar(0)
+        nc.sync.dma_start(out=e_codes[:].bitcast(I32), in_=enc_words.rearrange("k p n -> p k n").bitcast(I32))
+        load_scale_rows(rs_first, radar_scales[:, :, :PASS])
+        load_scale_rows(e_scales, enc_scales)
+        load_scale_rows(rs_rest, radar_scales[:, :, PASS:])
+        load_radar(1)
+        load_camera(0)
+        load_camera(1)
+        load_radar(2)
+        load_align_scales()
+        load_radar(3)
+        load_align(0)
+        load_w(0)
+        load_w(1)
+        for c in range(1, T // CHUNK):
+            load_camera(2 * c)
+            load_camera(2 * c + 1)
+            load_align(c)
+
+        r_codes, r_scales, h_rows, h_codes, h_scales = {}, {}, {}, {}, {}
+        w_rows, w_codes, w_scales = {}, {}, {}
+        cam_sorted, cam_rows, cam_codes, cam_scales = {}, {}, {}, {}
+        h_bank, t_bank, acc = {}, {}, {}
+
+        def deal(g):
+            r_codes[g] = kept("r_codes%d" % g, [P, PACK, KP, P], U16)
+            nc.vector.tensor_copy(
+                out=r_codes[g][:].rearrange("p t k (b i) -> p k b t i", i=8),
+                in_=r_raw[g][:].bitcast(U16).rearrange("p k (b i t) -> p k b t i", i=8, t=PACK),
+            )
+            r_scales[g] = kept("r_scales%d" % g, [P, PACK, KP, P], U8)
+            raw = rs_first[:] if g == 0 else rs_rest[:, :, PASS * (g - 1) : PASS * g]
+            nc.vector.tensor_copy(
+                out=r_scales[g][:].rearrange("p t k (b i) -> p k b t i", i=16),
+                in_=raw.rearrange("p k (b i t) -> p k b t i", i=16, t=PACK),
+            )
+
+        def encode(g, q):
+            h_bank[g, q] = work_bank()
+            for t in range(PACK):
+                for k in range(KP):
+                    nc.tensor.matmul_mx(
+                        out=h_bank[g, q][:, P * t : P * (t + 1)],
+                        lhsT=r_codes[g][:, t, k, :].bitcast(FP4X4),
+                        lhsT_scale=r_scales[g][:, t, k, :],
+                        rhs=e_codes[:, k, 2 * P * q : 2 * P * (q + 1)].bitcast(FP4X4),
+                        rhs_scale=e_scales[:, k, P * q : P * (q + 1)],
+                        start=(k == 0),
+                        stop=(k == KP - 1),
+                    )
+
+        def weigh(g, q):
+            if q == 0:
+                h_rows[g] = streamed("h_rows", [P, F, PACK], BF16)
+            nc.vector.scalar_tensor_tensor(
+                out=h_rows[g][:, P * q : P * (q + 1), :],
+                in0=h_bank[g, q][:].rearrange("p (t f) -> p f t", t=PACK),
+                scalar=0.0,
+                in1=trust_sb[:, g, :].unsqueeze(1).to_broadcast([P, P, PACK]),
+                op0=ALU.max,
+                op1=ALU.mult,
+            )
+
+        def quantise(rows, name, width):
+            codes = kept(name + "_codes", [P, width], U32)
+            scales = kept(name + "_scales", [P, width], U8)
+            nc.vector.quantize_mx(out=codes[:].bitcast(FP8X4), scales=scales[:], in_=rows)
+            return codes, scales
+
+        def quantise_h(g):
+            h_codes[g], h_scales[g] = quantise(h_rows[g][:].rearrange("p f t -> p (f t)"), "h%d" % g, F)
+
+        def interleave_w(k):
+            w_rows[k] = kept("w_rows%d" % k, [P, F, PACK], BF16)
+            nc.scalar.copy(
+                out=w_rows[k][:].rearrange("p (c i) t -> p c t i", i=4),
+                in_=w_raw[k][:].rearrange("p t (c i) -> p c t i", i=4),
+            )
+
+        def quantise_w(k):
+            w_codes[k], w_scales[k] = quantise(w_rows[k][:].rearrange("p f t -> p (f t)"), "w%d" % k, F)
+
+        def sort_camera(j):
+            cam_sorted[j] = streamed("cam_sorted", [P, DP, 2, P], F32)
+            words = cam_raw[j // 2][:, j % 2, :].bitcast(F32)
+            nc.scalar.copy(out=cam_sorted[j][:], in_=words.rearrange("p (k m u) -> p k u m", k=DP, u=2))
+
+        def turn_camera(j):
+            t_bank[j] = bank(4 + j) if j < EARLY else work_bank()
+            for k in range(DP):
+                for u in range(2):
+                    slot = 2 * k + u
+                    nc.tensor.transpose(t_bank[j][:, P * slot : P * (slot + 1)], cam_sorted[j][:, k, u, :], ident[:])
+
+        def gather_camera(j):
+            cam_rows[j] = streamed("cam_rows", [P, DP, P, 2], F32, 8)
+            nc.scalar.copy(out=cam_rows[j][:], in_=t_bank[j][:].rearrange("p (k u r) -> p k r u", k=DP, u=2))
+
+        def quantise_camera(j):
+            rows = cam_rows[j][:].rearrange("p k r u -> p (k r u)").bitcast(BF16)
+            cam_codes[j], cam_scales[j] = quantise(rows, "cam%d" % j, DP * P)
+
+        def move_pass(j, g, start, stop):
+            if start:
+                acc[j] = bank(4 + j % 4)
+            col = P * j % CHUNK
+            nc.tensor.matmul_mx(
+                out=acc[j][:],
+                lhsT=a_codes[P * j // CHUNK][:, g, col : col + P].bitcast(FP8X4),
+                lhsT_scale=a_scales[4 * g :, P * j : P * (j + 1)],
+                rhs=h_codes[g][:].bitcast(FP8X4),
+                rhs_scale=h_scales[g][:],
+                start=start,
+                stop=stop,
+            )
+
+        def camera_pass(j, k, stop):
+            nc.tensor.matmul_mx(
+                out=acc[j][:],
+                lhsT=cam_codes[j][:, P * k : P * (k + 1)].bitcast(FP8X4),
+                lhsT_scale=cam_scales[j][:, P * k : P * (k + 1)],
+                rhs=w_codes[k][:].bitcast(FP8X4),
+                rhs_scale=w_scales[k][:],
+                start=False,
+                stop=stop,
+            )
+
+        def spread_bias():
+            spread = work_bank()
+            words = bias_col[:].bitcast(F32)
+            for u in range(2):
+                nc.tensor.transpose(spread[:, P * u : P * (u + 1)], words[:, u : u + 1].to_broadcast([P, P]), ident[:])
+            rows = kept("bias_rows", [P, F], BF16)
+            nc.scalar.copy(
+                out=rows[:].bitcast(F32).rearrange("p (m u) -> p m u", u=2),
+                in_=spread[:, : 2 * P].rearrange("p (u m) -> p m u", u=2),
+            )
+            return rows
+
+        def finish(j):
+            result = streamed("result", [P, F], F32)
+            nc.vector.tensor_tensor(out=result[:], in0=acc[j][:], in1=bias_rows[:], op=ALU.add)
+            nc.sync.dma_start(out=out[P * j : P * (j + 1), :], in_=result[:])
+
+        def last_tile(j):
+            col = P * j % CHUNK
+            for half in range(2):
+                cols = slice(half * F // 2, (half + 1) * F // 2)
+                part = work_bank()
+                for g in range(MP):
+                    nc.tensor.matmul_mx(
+                        out=part[:, : F // 2],
+                        lhsT=a_codes[P * j // CHUNK][:, g, col : col + P].bitcast(FP8X4),
+                        lhsT_scale=a_scales[4 * g :, P * j : P * (j + 1)],
+                        rhs=h_codes[g][:, cols].bitcast(FP8X4),
+                        rhs_scale=h_scales[g][:, cols],
+                        start=(g == 0),
+                        stop=False,
+                    )
+                for k in range(DP):
+                    nc.tensor.matmul_mx(
+                        out=part[:, : F // 2],
+                        lhsT=cam_codes[j][:, P * k : P * (k + 1)].bitcast(FP8X4),
+                        lhsT_scale=cam_scales[j][:, P * k : P * (k + 1)],
+                        rhs=w_codes[k][:, cols].bitcast(FP8X4),
+                        rhs_scale=w_scales[k][:, cols],
+                        start=False,
+                        stop=(k == DP - 1),
+                    )
+                halves.append((part, cols))
+
+        def finish_half(j, part, cols):
+            result = streamed("result", [P, F // 2], F32)
+            nc.vector.tensor_tensor(out=result[:], in0=part[:, : F // 2], in1=bias_rows[:, cols], op=ALU.add)
+            nc.sync.dma_start(out=out[P * j : P * (j + 1), cols], in_=result[:])
+
+        halves = []
+        early = range(EARLY)
+        deal(0)
+        for q in range(QUARTERS):
+            encode(0, q)
+        deal(1)
+        for j in early:
+            sort_camera(j)
+        for q in range(QUARTERS):
+            weigh(0, q)
+            encode(1, q)
+        for j in early:
+            turn_camera(j)
+        deal(2)
+        for q in range(QUARTERS):
+            weigh(1, q)
+            encode(2, q)
+        for j in early:
+            gather_camera(j)
+        quantise_h(0)
+        deal(3)
+        quantise_h(1)
+        for g in range(2):
+            for j in early:
+                move_pass(j, g, g == 0, False)
+        interleave_w(0)
+        for q in range(QUARTERS):
+            weigh(2, q)
+            encode(3, q)
+        interleave_w(1)
+        for j in early:
+            quantise_camera(j)
+        quantise_h(2)
+        quantise_w(0)
+        for j in early:
+            move_pass(j, 2, False, False)
+        for j in early:
+            camera_pass(j, 0, False)
+        for j in range(EARLY, 2 * EARLY):
+            sort_camera(j)
+        quantise_w(1)
+        for q in range(QUARTERS):
+            weigh(3, q)
+        for j in early:
+            camera_pass(j, 1, False)
+        bias_rows = spread_bias()
+        for j in range(EARLY, 2 * EARLY):
+            turn_camera(j)
+            gather_camera(j)
+        quantise_h(3)
+        for j in early:
+            move_pass(j, 3, False, True)
+        for first in range(EARLY, TILES, EARLY):
+            ahead = range(first + EARLY, min(first + 2 * EARLY, TILES))
+            for j in ahead:
+                sort_camera(j)
+            for j in range(first, first + EARLY):
+                quantise_camera(j)
+                finish(j - EARLY)
+                if j == TILES - 1:
+                    last_tile(j)
+                else:
+                    for g in range(MP):
+                        move_pass(j, g, g == 0, False)
+                    for k in range(DP):
+                        camera_pass(j, k, k == DP - 1)
+                if j == first + 1:
+                    for i in ahead:
+                        turn_camera(i)
+                        gather_camera(i)
+        for j in range(TILES - EARLY, TILES - 1):
+            finish(j)
+        for part, cols in halves:
+            finish_half(TILES - 1, part, cols)

@@ -26,6 +26,8 @@ TILES = T // P
 QUARTERS = F // P
 CHUNK = 512
 EARLY = 4
+BANKS = 8
+HALF = F // 2
 
 
 def tile_radar_camera_fusion_s4_kernel(
@@ -47,15 +49,14 @@ def tile_radar_camera_fusion_s4_kernel(
         def bank(index):
             return psum.tile([P, F], F32, name="bank%d" % index)
 
-        work_count = []
+        ring = []
 
-        def work_bank():
-            work_count.append(0)
-            return bank((len(work_count) - 1) % 4)
+        def next_bank():
+            ring.append(0)
+            return bank((len(ring) - 1) % BANKS)
 
         r_raw = [kept("r_raw%d" % g, [P, KP, 2 * PASS], U8) for g in range(MP)]
-        rs_first = kept("rs_first", [P, KP, PASS], U8)
-        rs_rest = kept("rs_rest", [P, KP, M - PASS], U8)
+        rs_raw = [kept("rs_raw%d" % h, [P, KP, M // 2], U8) for h in range(2)]
         e_codes = kept("e_codes", [P, KP, 2 * F], U8)
         e_scales = kept("e_scales", [P, KP, F], U8)
         a_codes = [kept("a_codes%d" % c, [P, MP, CHUNK], U32) for c in range(T // CHUNK)]
@@ -66,13 +67,11 @@ def tile_radar_camera_fusion_s4_kernel(
         bias_col = kept("bias_col", [P, PACK], BF16)
         ident = kept("ident", [P, P], F32)
 
-        nc.vector.memset(rs_first[:].rearrange("p k n -> p (k n)").bitcast(I32), 0)
+        nc.vector.memset(rs_raw[0][:].rearrange("p k n -> p (k n)").bitcast(I32), 0)
         nc.vector.memset(e_scales[:].rearrange("p k n -> p (k n)").bitcast(I32), 0)
-        nc.vector.memset(rs_rest[:].rearrange("p k n -> p (k n)").bitcast(I32), 0)
+        nc.vector.memset(rs_raw[1][:].rearrange("p k n -> p (k n)").bitcast(I32), 0)
         nc.vector.memset(a_scales[:].bitcast(I32), 0)
-        nc.gpsimd.dma_start(out=trust_sb[:], in_=trust.rearrange("(g p t) -> p g t", p=P, t=PACK))
         make_identity(nc, ident[:])
-        nc.gpsimd.dma_start(out=bias_col[:], in_=bias.rearrange("(p t) -> p t", t=PACK))
 
         def load_radar(g):
             src = radar_words[:, :, 2 * PASS * g : 2 * PASS * (g + 1)].rearrange("k p n -> p k n")
@@ -101,20 +100,25 @@ def tile_radar_camera_fusion_s4_kernel(
             nc.sync.dma_start(out=w_raw[k][:], in_=src)
 
         load_radar(0)
+        load_scale_rows(rs_raw[0], radar_scales[:, :, : M // 2])
         nc.sync.dma_start(out=e_codes[:].bitcast(I32), in_=enc_words.rearrange("k p n -> p k n").bitcast(I32))
-        load_scale_rows(rs_first, radar_scales[:, :, :PASS])
         load_scale_rows(e_scales, enc_scales)
-        load_scale_rows(rs_rest, radar_scales[:, :, PASS:])
         load_radar(1)
+        nc.sync.dma_start(out=trust_sb[:], in_=trust.rearrange("(g p t) -> p g t", p=P, t=PACK))
+        load_scale_rows(rs_raw[1], radar_scales[:, :, M // 2 :])
         load_camera(0)
-        load_camera(1)
         load_radar(2)
+        nc.sync.dma_start(out=bias_col[:], in_=bias.rearrange("(p t) -> p t", t=PACK))
+        load_camera(1)
         load_align_scales()
         load_radar(3)
         load_align(0)
         load_w(0)
+        load_camera(2)
+        load_camera(3)
         load_w(1)
-        for c in range(1, T // CHUNK):
+        load_align(1)
+        for c in range(2, T // CHUNK):
             load_camera(2 * c)
             load_camera(2 * c + 1)
             load_align(c)
@@ -122,23 +126,59 @@ def tile_radar_camera_fusion_s4_kernel(
         r_codes, r_scales, h_rows, h_codes, h_scales = {}, {}, {}, {}, {}
         w_rows, w_codes, w_scales = {}, {}, {}
         cam_sorted, cam_rows, cam_codes, cam_scales = {}, {}, {}, {}
-        h_bank, t_bank, acc = {}, {}, {}
+        h_bank, t_bank, acc, h_pairs = {}, {}, {}, {}
 
-        def deal(g):
+        def deal_codes(g):
             r_codes[g] = kept("r_codes%d" % g, [P, PACK, KP, P], U16)
             nc.vector.tensor_copy(
                 out=r_codes[g][:].rearrange("p t k (b i) -> p k b t i", i=8),
                 in_=r_raw[g][:].bitcast(U16).rearrange("p k (b i t) -> p k b t i", i=8, t=PACK),
             )
+
+        def deal_scales(g):
             r_scales[g] = kept("r_scales%d" % g, [P, PACK, KP, P], U8)
-            raw = rs_first[:] if g == 0 else rs_rest[:, :, PASS * (g - 1) : PASS * g]
+            raw = rs_raw[g // 2][:, :, PASS * (g % 2) : PASS * (g % 2 + 1)]
             nc.vector.tensor_copy(
                 out=r_scales[g][:].rearrange("p t k (b i) -> p k b t i", i=16),
                 in_=raw.rearrange("p k (b i t) -> p k b t i", i=16, t=PACK),
             )
 
         def encode(g, q):
-            h_bank[g, q] = work_bank()
+            half, u = divmod(q, 2)
+            h_bank[g, q] = next_bank()
+            for e in range(2):
+                for k in range(KP):
+                    nc.tensor.matmul_mx(
+                        out=h_bank[g, q][:, HALF * e : HALF * (e + 1)],
+                        lhsT=r_codes[g][:, 2 * u + e, k, :].bitcast(FP4X4),
+                        lhsT_scale=r_scales[g][:, 2 * u + e, k, :],
+                        rhs=e_codes[:, k, 2 * HALF * half : 2 * HALF * (half + 1)].bitcast(FP4X4),
+                        rhs_scale=e_scales[:, k, HALF * half : HALF * (half + 1)],
+                        start=(k == 0),
+                        stop=(k == KP - 1),
+                    )
+
+        def weigh(g, q):
+            half, u = divmod(q, 2)
+            if u == 0:
+                h_pairs[g, half] = streamed("h_pairs", [P, 2, HALF, 2], BF16)
+            nc.vector.scalar_tensor_tensor(
+                out=h_pairs[g, half][:, u, :, :],
+                in0=h_bank[g, q][:].rearrange("p (e f) -> p f e", e=2),
+                scalar=0.0,
+                in1=trust_sb[:, g, 2 * u : 2 * u + 2].unsqueeze(1).to_broadcast([P, HALF, 2]),
+                op0=ALU.max,
+                op1=ALU.mult,
+            )
+
+        def merge(g, half):
+            if half == 0:
+                h_rows[g] = streamed("h_rows", [P, F, 2], F32, 2)
+            words = h_pairs[g, half][:].rearrange("p u f e -> p u (f e)").bitcast(F32)
+            nc.scalar.copy(out=h_rows[g][:, HALF * half : HALF * (half + 1), :], in_=words.rearrange("p u f -> p f u"))
+
+        def encode_narrow(g, q):
+            h_bank[g, q] = next_bank()
             for t in range(PACK):
                 for k in range(KP):
                     nc.tensor.matmul_mx(
@@ -151,11 +191,12 @@ def tile_radar_camera_fusion_s4_kernel(
                         stop=(k == KP - 1),
                     )
 
-        def weigh(g, q):
+        def weigh_narrow(g, q):
             if q == 0:
-                h_rows[g] = streamed("h_rows", [P, F, PACK], BF16)
+                h_rows[g] = streamed("h_rows", [P, F, 2], F32, 2)
+            rows = h_rows[g][:].rearrange("p f u -> p (f u)").bitcast(BF16).rearrange("p (f t) -> p f t", t=PACK)
             nc.vector.scalar_tensor_tensor(
-                out=h_rows[g][:, P * q : P * (q + 1), :],
+                out=rows[:, P * q : P * (q + 1), :],
                 in0=h_bank[g, q][:].rearrange("p (t f) -> p f t", t=PACK),
                 scalar=0.0,
                 in1=trust_sb[:, g, :].unsqueeze(1).to_broadcast([P, P, PACK]),
@@ -170,11 +211,11 @@ def tile_radar_camera_fusion_s4_kernel(
             return codes, scales
 
         def quantise_h(g):
-            h_codes[g], h_scales[g] = quantise(h_rows[g][:].rearrange("p f t -> p (f t)"), "h%d" % g, F)
+            h_codes[g], h_scales[g] = quantise(h_rows[g][:].rearrange("p f u -> p (f u)").bitcast(BF16), "h%d" % g, F)
 
-        def interleave_w(k):
+        def interleave_w(k, copy):
             w_rows[k] = kept("w_rows%d" % k, [P, F, PACK], BF16)
-            nc.scalar.copy(
+            copy(
                 out=w_rows[k][:].rearrange("p (c i) t -> p c t i", i=4),
                 in_=w_raw[k][:].rearrange("p t (c i) -> p c t i", i=4),
             )
@@ -188,7 +229,7 @@ def tile_radar_camera_fusion_s4_kernel(
             nc.scalar.copy(out=cam_sorted[j][:], in_=words.rearrange("p (k m u) -> p k u m", k=DP, u=2))
 
         def turn_camera(j):
-            t_bank[j] = bank(4 + j) if j < EARLY else work_bank()
+            t_bank[j] = next_bank()
             for k in range(DP):
                 for u in range(2):
                     slot = 2 * k + u
@@ -204,7 +245,7 @@ def tile_radar_camera_fusion_s4_kernel(
 
         def move_pass(j, g, start, stop):
             if start:
-                acc[j] = bank(4 + j % 4)
+                acc[j] = next_bank()
             col = P * j % CHUNK
             nc.tensor.matmul_mx(
                 out=acc[j][:],
@@ -228,7 +269,7 @@ def tile_radar_camera_fusion_s4_kernel(
             )
 
         def spread_bias():
-            spread = work_bank()
+            spread = bank(0)
             words = bias_col[:].bitcast(F32)
             for u in range(2):
                 nc.tensor.transpose(spread[:, P * u : P * (u + 1)], words[:, u : u + 1].to_broadcast([P, P]), ident[:])
@@ -248,7 +289,7 @@ def tile_radar_camera_fusion_s4_kernel(
             col = P * j % CHUNK
             for half in range(2):
                 cols = slice(half * F // 2, (half + 1) * F // 2)
-                part = work_bank()
+                part = next_bank()
                 for g in range(MP):
                     nc.tensor.matmul_mx(
                         out=part[:, : F // 2],
@@ -278,75 +319,99 @@ def tile_radar_camera_fusion_s4_kernel(
 
         halves = []
         early = range(EARLY)
-        deal(0)
-        for q in range(QUARTERS):
-            encode(0, q)
-        deal(1)
+        second = range(EARLY, 2 * EARLY)
+
+        def encode_all(g, form):
+            for q in range(QUARTERS):
+                form(g, q)
+
+        def weigh_all(g, form):
+            for q in range(QUARTERS):
+                form(g, q)
+
+        def merge_all(g):
+            for half in range(2):
+                merge(g, half)
+
+        def moves(tiles, g):
+            for j in tiles:
+                move_pass(j, g, g == 0, False)
+
+        deal_codes(0)
+        deal_scales(0)
+        deal_scales(1)
+        deal_codes(1)
+        encode_all(0, encode_narrow)
+        encode_all(1, encode_narrow)
         for j in early:
             sort_camera(j)
-        for q in range(QUARTERS):
-            weigh(0, q)
-            encode(1, q)
+        weigh_all(0, weigh_narrow)
         for j in early:
             turn_camera(j)
-        deal(2)
-        for q in range(QUARTERS):
-            weigh(1, q)
-            encode(2, q)
-        for j in early:
             gather_camera(j)
+        bias_rows = spread_bias()
+        deal_scales(2)
+        deal_codes(2)
+        weigh_all(1, weigh_narrow)
+        encode_all(2, encode_narrow)
         quantise_h(0)
-        deal(3)
+        moves(early, 0)
+        deal_scales(3)
         quantise_h(1)
-        for g in range(2):
-            for j in early:
-                move_pass(j, g, g == 0, False)
-        interleave_w(0)
-        for q in range(QUARTERS):
-            weigh(2, q)
-            encode(3, q)
-        interleave_w(1)
-        for j in early:
-            quantise_camera(j)
+        moves(early, 1)
+        deal_codes(3)
+        interleave_w(0, nc.scalar.copy)
+        weigh_all(2, weigh_narrow)
+        encode_all(3, encode_narrow)
+        for j in second:
+            sort_camera(j)
+        interleave_w(1, nc.scalar.copy)
         quantise_h(2)
+        moves(early, 2)
+        weigh_all(3, weigh_narrow)
+        ring.extend([0] * EARLY)
+        for j in second:
+            turn_camera(j)
+            gather_camera(j)
+        quantise_camera(0)
+        quantise_h(3)
+        moves(early, 3)
+        quantise_camera(1)
+        quantise_camera(2)
+        quantise_camera(3)
         quantise_w(0)
-        for j in early:
-            move_pass(j, 2, False, False)
+        ring.extend([0] * EARLY)
+        for g in range(MP):
+            moves([EARLY], g)
         for j in early:
             camera_pass(j, 0, False)
-        for j in range(EARLY, 2 * EARLY):
-            sort_camera(j)
+        quantise_camera(EARLY)
         quantise_w(1)
-        for q in range(QUARTERS):
-            weigh(3, q)
         for j in early:
-            camera_pass(j, 1, False)
-        bias_rows = spread_bias()
-        for j in range(EARLY, 2 * EARLY):
-            turn_camera(j)
-            gather_camera(j)
-        quantise_h(3)
-        for j in early:
-            move_pass(j, 3, False, True)
-        for first in range(EARLY, TILES, EARLY):
-            ahead = range(first + EARLY, min(first + 2 * EARLY, TILES))
-            for j in ahead:
-                sort_camera(j)
-            for j in range(first, first + EARLY):
-                quantise_camera(j)
-                finish(j - EARLY)
-                if j == TILES - 1:
-                    last_tile(j)
-                else:
-                    for g in range(MP):
-                        move_pass(j, g, g == 0, False)
-                    for k in range(DP):
-                        camera_pass(j, k, k == DP - 1)
-                if j == first + 1:
-                    for i in ahead:
-                        turn_camera(i)
-                        gather_camera(i)
-        for j in range(TILES - EARLY, TILES - 1):
-            finish(j)
+            camera_pass(j, 1, True)
+        for k in range(DP):
+            camera_pass(EARLY, k, k == DP - 1)
+        for j in range(2 * EARLY, 3 * EARLY):
+            sort_camera(j)
+        done = []
+        for j in range(EARLY + 1, TILES):
+            quantise_camera(j)
+            for i in range(len(done), j - 1):
+                finish(i)
+                done.append(i)
+            if j == TILES - 1:
+                last_tile(j)
+            else:
+                for g in range(MP):
+                    move_pass(j, g, g == 0, False)
+                for k in range(DP):
+                    camera_pass(j, k, k == DP - 1)
+            if j % EARLY == 2 and j + 2 < TILES:
+                for i in range(j + 2, j + 2 + EARLY):
+                    turn_camera(i)
+                    gather_camera(i)
+                for i in range(j + 2 + EARLY, min(j + 2 + 2 * EARLY, TILES)):
+                    sort_camera(i)
+        finish(TILES - 2)
         for part, cols in halves:
             finish_half(TILES - 1, part, cols)

@@ -19,15 +19,19 @@ ALU = mybir.AluOpType
 P = 128
 PACK = 4
 PASS = P * PACK
-KP = K // PASS
-MP = M // PASS
-DP = D // PASS
+RADAR_PASSES = K // PASS
+GROUPS = M // PASS
+CAMERA_PASSES = D // PASS
 TILES = T // P
 QUARTERS = F // P
+QUADRANTS = 4
 CHUNK = 512
-EARLY = 4
+PAIR = 2
+LINE = 16
 BANKS = 8
-HALF = F // 2
+RUN = BANKS // 2
+OPENED = RUN + 2
+DEPTH = 2 * RUN
 
 
 def tile_radar_camera_fusion_s4_kernel(
@@ -36,34 +40,28 @@ def tile_radar_camera_fusion_s4_kernel(
     nc = tc.nc
     with ExitStack() as ctx:
         keep = ctx.enter_context(tc.tile_pool(name="keep", bufs=1))
-        stream = ctx.enter_context(tc.tile_pool(name="stream", bufs=4))
+        stream = ctx.enter_context(tc.tile_pool(name="stream", bufs=RUN))
         psum = ctx.enter_context(tc.psum_pool(name="psum", bufs=1))
         ctx.enter_context(tc.manual_schedule())
 
         def kept(name, shape, dtype):
             return keep.tile(shape, dtype, name=name, align_bytes=64)
 
-        def streamed(name, shape, dtype, bufs=4):
+        def streamed(name, shape, dtype, bufs):
             return stream.tile(shape, dtype, name=name, bufs=bufs, align_bytes=64)
 
         def bank(index):
             return psum.tile([P, F], F32, name="bank%d" % index)
 
-        ring = []
-
-        def next_bank():
-            ring.append(0)
-            return bank((len(ring) - 1) % BANKS)
-
-        r_raw = [kept("r_raw%d" % g, [P, KP, 2 * PASS], U8) for g in range(MP)]
-        rs_raw = [kept("rs_raw%d" % h, [P, KP, M // 2], U8) for h in range(2)]
-        e_codes = kept("e_codes", [P, KP, 2 * F], U8)
-        e_scales = kept("e_scales", [P, KP, F], U8)
-        a_codes = [kept("a_codes%d" % c, [P, MP, CHUNK], U32) for c in range(T // CHUNK)]
+        r_raw = [kept("r_raw%d" % g, [P, RADAR_PASSES, 2 * PASS], U8) for g in range(GROUPS)]
+        rs_raw = [kept("rs_raw%d" % h, [P, RADAR_PASSES, PAIR * PASS], U8) for h in range(GROUPS // PAIR)]
+        e_codes = kept("e_codes", [P, RADAR_PASSES, 2 * F], U8)
+        e_scales = kept("e_scales", [P, RADAR_PASSES, F], U8)
+        a_codes = [kept("a_codes%d" % c, [P, GROUPS, CHUNK], U32) for c in range(T // CHUNK)]
         a_scales = kept("a_scales", [P, T], U8)
-        cam_raw = [kept("cam_raw%d" % c, [P, 2, D], BF16) for c in range(TILES // 2)]
-        w_raw = [kept("w_raw%d" % k, [P, PACK, F], BF16) for k in range(DP)]
-        trust_sb = kept("trust_sb", [P, MP, PACK], BF16)
+        cam_raw = [kept("cam_raw%d" % c, [P, PAIR, D], BF16) for c in range(TILES // PAIR)]
+        w_raw = [kept("w_raw%d" % k, [P, PACK, F], BF16) for k in range(CAMERA_PASSES)]
+        trust_sb = kept("trust_sb", [P, GROUPS, PACK], BF16)
         bias_col = kept("bias_col", [P, PACK], BF16)
         ident = kept("ident", [P, P], F32)
 
@@ -78,12 +76,15 @@ def tile_radar_camera_fusion_s4_kernel(
             nc.sync.dma_start(out=r_raw[g][:].bitcast(I32), in_=src.bitcast(I32))
 
         def load_scale_rows(plane, rows):
-            for q in range(4):
+            for q in range(QUADRANTS):
                 src = rows[:, 4 * q : 4 * q + 4, :].rearrange("k r n -> r k n")
                 nc.sync.dma_start(out=plane[32 * q : 32 * q + 4, :, :].bitcast(I32), in_=src.bitcast(I32))
 
+        def load_radar_scales(h):
+            load_scale_rows(rs_raw[h], radar_scales[:, :, PAIR * PASS * h : PAIR * PASS * (h + 1)])
+
         def load_align_scales():
-            for q in range(4):
+            for q in range(QUADRANTS):
                 src = align_scales[:, 4 * q : 4 * q + 4, :]
                 nc.sync.dma_start(out=a_scales[32 * q : 32 * q + 16, :].bitcast(I32), in_=src.bitcast(I32))
 
@@ -92,117 +93,85 @@ def tile_radar_camera_fusion_s4_kernel(
             nc.sync.dma_start(out=a_codes[c][:].bitcast(I32), in_=src.bitcast(I32))
 
         def load_camera(c):
-            src = camera[2 * P * c : 2 * P * (c + 1), :].rearrange("(j p) d -> p j d", p=P)
+            src = camera[PAIR * P * c : PAIR * P * (c + 1), :].rearrange("(j p) d -> p j d", p=P)
             nc.sync.dma_start(out=cam_raw[c][:], in_=src)
 
         def load_w(k):
-            src = w_cam[PASS * k : PASS * (k + 1), :].rearrange("(p j) f -> p j f", j=PACK)
+            src = w_cam[PASS * k : PASS * (k + 1), :].rearrange("(p t) f -> p t f", t=PACK)
             nc.sync.dma_start(out=w_raw[k][:], in_=src)
 
         load_radar(0)
-        load_scale_rows(rs_raw[0], radar_scales[:, :, : M // 2])
+        load_radar_scales(0)
         nc.sync.dma_start(out=e_codes[:].bitcast(I32), in_=enc_words.rearrange("k p n -> p k n").bitcast(I32))
         load_scale_rows(e_scales, enc_scales)
         load_radar(1)
         nc.sync.dma_start(out=trust_sb[:], in_=trust.rearrange("(g p t) -> p g t", p=P, t=PACK))
-        load_scale_rows(rs_raw[1], radar_scales[:, :, M // 2 :])
+        load_radar_scales(1)
         load_camera(0)
+        load_camera(1)
         load_radar(2)
         nc.sync.dma_start(out=bias_col[:], in_=bias.rearrange("(p t) -> p t", t=PACK))
-        load_camera(1)
         load_align_scales()
         load_radar(3)
         load_align(0)
         load_w(0)
         load_camera(2)
         load_camera(3)
-        load_w(1)
         load_align(1)
+        load_w(1)
         for c in range(2, T // CHUNK):
             load_camera(2 * c)
             load_camera(2 * c + 1)
             load_align(c)
 
-        r_codes, r_scales, h_rows, h_codes, h_scales = {}, {}, {}, {}, {}
+        r_codes, r_scales = {}, {}
+        h_bank, h_rows, h_codes, h_scales = {}, {}, {}, {}
         w_rows, w_codes, w_scales = {}, {}, {}
         cam_sorted, cam_rows, cam_codes, cam_scales = {}, {}, {}, {}
-        h_bank, t_bank, acc, h_pairs = {}, {}, {}, {}
+        acc = {}
 
         def deal_codes(g):
-            r_codes[g] = kept("r_codes%d" % g, [P, PACK, KP, P], U16)
+            r_codes[g] = kept("r_codes%d" % g, [P, PACK, RADAR_PASSES, P], U16)
             nc.vector.tensor_copy(
-                out=r_codes[g][:].rearrange("p t k (b i) -> p k b t i", i=8),
-                in_=r_raw[g][:].bitcast(U16).rearrange("p k (b i t) -> p k b t i", i=8, t=PACK),
+                out=r_codes[g][:].rearrange("p t k (b i) -> p k b t i", i=LINE // 2),
+                in_=r_raw[g][:].bitcast(U16).rearrange("p k (b i t) -> p k b t i", i=LINE // 2, t=PACK),
             )
 
         def deal_scales(g):
-            r_scales[g] = kept("r_scales%d" % g, [P, PACK, KP, P], U8)
-            raw = rs_raw[g // 2][:, :, PASS * (g % 2) : PASS * (g % 2 + 1)]
+            r_scales[g] = kept("r_scales%d" % g, [P, PACK, RADAR_PASSES, P], U8)
+            raw = rs_raw[g // PAIR][:, :, PASS * (g % PAIR) : PASS * (g % PAIR + 1)]
             nc.vector.tensor_copy(
-                out=r_scales[g][:].rearrange("p t k (b i) -> p k b t i", i=16),
-                in_=raw.rearrange("p k (b i t) -> p k b t i", i=16, t=PACK),
+                out=r_scales[g][:].rearrange("p t k (b i) -> p k b t i", i=LINE),
+                in_=raw.rearrange("p k (b i t) -> p k b t i", i=LINE, t=PACK),
             )
 
-        def encode(g, q):
-            half, u = divmod(q, 2)
-            h_bank[g, q] = next_bank()
-            for e in range(2):
-                for k in range(KP):
-                    nc.tensor.matmul_mx(
-                        out=h_bank[g, q][:, HALF * e : HALF * (e + 1)],
-                        lhsT=r_codes[g][:, 2 * u + e, k, :].bitcast(FP4X4),
-                        lhsT_scale=r_scales[g][:, 2 * u + e, k, :],
-                        rhs=e_codes[:, k, 2 * HALF * half : 2 * HALF * (half + 1)].bitcast(FP4X4),
-                        rhs_scale=e_scales[:, k, HALF * half : HALF * (half + 1)],
-                        start=(k == 0),
-                        stop=(k == KP - 1),
-                    )
+        def encode(g, first_bank):
+            for q in range(QUARTERS):
+                h_bank[g, q] = bank(first_bank + q)
+                for t in range(PACK):
+                    for k in range(RADAR_PASSES):
+                        nc.tensor.matmul_mx(
+                            out=h_bank[g, q][:, P * t : P * (t + 1)],
+                            lhsT=r_codes[g][:, t, k, :].bitcast(FP4X4),
+                            lhsT_scale=r_scales[g][:, t, k, :],
+                            rhs=e_codes[:, k, 2 * P * q : 2 * P * (q + 1)].bitcast(FP4X4),
+                            rhs_scale=e_scales[:, k, P * q : P * (q + 1)],
+                            start=(k == 0),
+                            stop=(k == RADAR_PASSES - 1),
+                        )
 
-        def weigh(g, q):
-            half, u = divmod(q, 2)
-            if u == 0:
-                h_pairs[g, half] = streamed("h_pairs", [P, 2, HALF, 2], BF16)
-            nc.vector.scalar_tensor_tensor(
-                out=h_pairs[g, half][:, u, :, :],
-                in0=h_bank[g, q][:].rearrange("p (e f) -> p f e", e=2),
-                scalar=0.0,
-                in1=trust_sb[:, g, 2 * u : 2 * u + 2].unsqueeze(1).to_broadcast([P, HALF, 2]),
-                op0=ALU.max,
-                op1=ALU.mult,
-            )
-
-        def merge(g, half):
-            if half == 0:
-                h_rows[g] = streamed("h_rows", [P, F, 2], F32, 2)
-            words = h_pairs[g, half][:].rearrange("p u f e -> p u (f e)").bitcast(F32)
-            nc.scalar.copy(out=h_rows[g][:, HALF * half : HALF * (half + 1), :], in_=words.rearrange("p u f -> p f u"))
-
-        def encode_narrow(g, q):
-            h_bank[g, q] = next_bank()
-            for t in range(PACK):
-                for k in range(KP):
-                    nc.tensor.matmul_mx(
-                        out=h_bank[g, q][:, P * t : P * (t + 1)],
-                        lhsT=r_codes[g][:, t, k, :].bitcast(FP4X4),
-                        lhsT_scale=r_scales[g][:, t, k, :],
-                        rhs=e_codes[:, k, 2 * P * q : 2 * P * (q + 1)].bitcast(FP4X4),
-                        rhs_scale=e_scales[:, k, P * q : P * (q + 1)],
-                        start=(k == 0),
-                        stop=(k == KP - 1),
-                    )
-
-        def weigh_narrow(g, q):
-            if q == 0:
-                h_rows[g] = streamed("h_rows", [P, F, 2], F32, 2)
-            rows = h_rows[g][:].rearrange("p f u -> p (f u)").bitcast(BF16).rearrange("p (f t) -> p f t", t=PACK)
-            nc.vector.scalar_tensor_tensor(
-                out=rows[:, P * q : P * (q + 1), :],
-                in0=h_bank[g, q][:].rearrange("p (t f) -> p f t", t=PACK),
-                scalar=0.0,
-                in1=trust_sb[:, g, :].unsqueeze(1).to_broadcast([P, P, PACK]),
-                op0=ALU.max,
-                op1=ALU.mult,
-            )
+        def weigh(g, quarters):
+            for q in quarters:
+                if q == 0:
+                    h_rows[g] = streamed("h_rows", [P, F, PACK], BF16, 2)
+                nc.vector.scalar_tensor_tensor(
+                    out=h_rows[g][:, P * q : P * (q + 1), :],
+                    in0=h_bank[g, q][:].rearrange("p (t f) -> p f t", t=PACK),
+                    scalar=0.0,
+                    in1=trust_sb[:, g, :].unsqueeze(1).to_broadcast([P, P, PACK]),
+                    op0=ALU.max,
+                    op1=ALU.mult,
+                )
 
         def quantise(rows, name, width):
             codes = kept(name + "_codes", [P, width], U32)
@@ -211,7 +180,7 @@ def tile_radar_camera_fusion_s4_kernel(
             return codes, scales
 
         def quantise_h(g):
-            h_codes[g], h_scales[g] = quantise(h_rows[g][:].rearrange("p f u -> p (f u)").bitcast(BF16), "h%d" % g, F)
+            h_codes[g], h_scales[g] = quantise(h_rows[g][:].rearrange("p f t -> p (f t)"), "h%d" % g, F)
 
         def interleave_w(k, copy):
             w_rows[k] = kept("w_rows%d" % k, [P, F, PACK], BF16)
@@ -223,56 +192,35 @@ def tile_radar_camera_fusion_s4_kernel(
         def quantise_w(k):
             w_codes[k], w_scales[k] = quantise(w_rows[k][:].rearrange("p f t -> p (f t)"), "w%d" % k, F)
 
-        def sort_camera(j):
-            cam_sorted[j] = streamed("cam_sorted", [P, DP, 2, P], F32)
-            words = cam_raw[j // 2][:, j % 2, :].bitcast(F32)
-            nc.scalar.copy(out=cam_sorted[j][:], in_=words.rearrange("p (k m u) -> p k u m", k=DP, u=2))
+        def sort_camera(tiles):
+            for j in tiles:
+                cam_sorted[j] = streamed("cam_sorted", [P, CAMERA_PASSES, 2, P], F32, RUN)
+                pairs = cam_raw[j // PAIR][:, j % PAIR, :].bitcast(F32)
+                nc.scalar.copy(
+                    out=cam_sorted[j][:], in_=pairs.rearrange("p (k m u) -> p k u m", k=CAMERA_PASSES, u=2)
+                )
 
-        def turn_camera(j):
-            t_bank[j] = next_bank()
-            for k in range(DP):
-                for u in range(2):
-                    slot = 2 * k + u
-                    nc.tensor.transpose(t_bank[j][:, P * slot : P * (slot + 1)], cam_sorted[j][:, k, u, :], ident[:])
-
-        def gather_camera(j):
-            cam_rows[j] = streamed("cam_rows", [P, DP, P, 2], F32, 8)
-            nc.scalar.copy(out=cam_rows[j][:], in_=t_bank[j][:].rearrange("p (k u r) -> p k r u", k=DP, u=2))
+        def turn_camera(tiles, first_bank):
+            for n, j in enumerate(tiles):
+                turned = bank((first_bank + n) % BANKS)
+                for k in range(CAMERA_PASSES):
+                    for u in range(2):
+                        cols = slice(P * (2 * k + u), P * (2 * k + u + 1))
+                        nc.tensor.transpose(turned[:, cols], cam_sorted[j][:, k, u, :], ident[:])
+                cam_rows[j] = streamed("cam_rows", [P, CAMERA_PASSES, P, 2], F32, DEPTH)
+                nc.scalar.copy(
+                    out=cam_rows[j][:], in_=turned[:].rearrange("p (k u r) -> p k r u", k=CAMERA_PASSES, u=2)
+                )
 
         def quantise_camera(j):
             rows = cam_rows[j][:].rearrange("p k r u -> p (k r u)").bitcast(BF16)
-            cam_codes[j], cam_scales[j] = quantise(rows, "cam%d" % j, DP * P)
+            cam_codes[j], cam_scales[j] = quantise(rows, "cam%d" % j, CAMERA_PASSES * P)
 
-        def move_pass(j, g, start, stop):
-            if start:
-                acc[j] = next_bank()
-            col = P * j % CHUNK
-            nc.tensor.matmul_mx(
-                out=acc[j][:],
-                lhsT=a_codes[P * j // CHUNK][:, g, col : col + P].bitcast(FP8X4),
-                lhsT_scale=a_scales[4 * g :, P * j : P * (j + 1)],
-                rhs=h_codes[g][:].bitcast(FP8X4),
-                rhs_scale=h_scales[g][:],
-                start=start,
-                stop=stop,
-            )
-
-        def camera_pass(j, k, stop):
-            nc.tensor.matmul_mx(
-                out=acc[j][:],
-                lhsT=cam_codes[j][:, P * k : P * (k + 1)].bitcast(FP8X4),
-                lhsT_scale=cam_scales[j][:, P * k : P * (k + 1)],
-                rhs=w_codes[k][:].bitcast(FP8X4),
-                rhs_scale=w_scales[k][:],
-                start=False,
-                stop=stop,
-            )
-
-        def spread_bias():
-            spread = bank(0)
-            words = bias_col[:].bitcast(F32)
+        def spread_bias(index):
+            spread = bank(index)
+            pairs = bias_col[:].bitcast(F32)
             for u in range(2):
-                nc.tensor.transpose(spread[:, P * u : P * (u + 1)], words[:, u : u + 1].to_broadcast([P, P]), ident[:])
+                nc.tensor.transpose(spread[:, P * u : P * (u + 1)], pairs[:, u : u + 1].to_broadcast([P, P]), ident[:])
             rows = kept("bias_rows", [P, F], BF16)
             nc.scalar.copy(
                 out=rows[:].bitcast(F32).rearrange("p (m u) -> p m u", u=2),
@@ -280,138 +228,132 @@ def tile_radar_camera_fusion_s4_kernel(
             )
             return rows
 
-        def finish(j):
-            result = streamed("result", [P, F], F32)
-            nc.vector.tensor_tensor(out=result[:], in0=acc[j][:], in1=bias_rows[:], op=ALU.add)
-            nc.sync.dma_start(out=out[P * j : P * (j + 1), :], in_=result[:])
+        def open_piece(piece, index):
+            whole_bank = bank(index)
+            acc[piece] = whole_bank[:, : piece[2] - piece[1]]
 
-        def last_tile(j):
+        def move_passes(piece, groups):
+            j, cols = piece[0], slice(piece[1], piece[2])
             col = P * j % CHUNK
-            for half in range(2):
-                cols = slice(half * F // 2, (half + 1) * F // 2)
-                part = next_bank()
-                for g in range(MP):
-                    nc.tensor.matmul_mx(
-                        out=part[:, : F // 2],
-                        lhsT=a_codes[P * j // CHUNK][:, g, col : col + P].bitcast(FP8X4),
-                        lhsT_scale=a_scales[4 * g :, P * j : P * (j + 1)],
-                        rhs=h_codes[g][:, cols].bitcast(FP8X4),
-                        rhs_scale=h_scales[g][:, cols],
-                        start=(g == 0),
-                        stop=False,
-                    )
-                for k in range(DP):
-                    nc.tensor.matmul_mx(
-                        out=part[:, : F // 2],
-                        lhsT=cam_codes[j][:, P * k : P * (k + 1)].bitcast(FP8X4),
-                        lhsT_scale=cam_scales[j][:, P * k : P * (k + 1)],
-                        rhs=w_codes[k][:, cols].bitcast(FP8X4),
-                        rhs_scale=w_scales[k][:, cols],
-                        start=False,
-                        stop=(k == DP - 1),
-                    )
-                halves.append((part, cols))
+            for g in groups:
+                nc.tensor.matmul_mx(
+                    out=acc[piece],
+                    lhsT=a_codes[P * j // CHUNK][:, g, col : col + P].bitcast(FP8X4),
+                    lhsT_scale=a_scales[4 * g :, P * j : P * (j + 1)],
+                    rhs=h_codes[g][:, cols].bitcast(FP8X4),
+                    rhs_scale=h_scales[g][:, cols],
+                    start=(g == 0),
+                    stop=False,
+                )
 
-        def finish_half(j, part, cols):
-            result = streamed("result", [P, F // 2], F32)
-            nc.vector.tensor_tensor(out=result[:], in0=part[:, : F // 2], in1=bias_rows[:, cols], op=ALU.add)
+        def camera_passes(piece, passes):
+            j, cols = piece[0], slice(piece[1], piece[2])
+            for k in passes:
+                nc.tensor.matmul_mx(
+                    out=acc[piece],
+                    lhsT=cam_codes[j][:, P * k : P * (k + 1)].bitcast(FP8X4),
+                    lhsT_scale=cam_scales[j][:, P * k : P * (k + 1)],
+                    rhs=w_codes[k][:, cols].bitcast(FP8X4),
+                    rhs_scale=w_scales[k][:, cols],
+                    start=False,
+                    stop=(k == CAMERA_PASSES - 1),
+                )
+
+        def finish(piece):
+            j, cols = piece[0], slice(piece[1], piece[2])
+            result = streamed("result", [P, piece[2] - piece[1]], F32, DEPTH)
+            nc.vector.tensor_tensor(out=result[:], in0=acc[piece], in1=bias_rows[:, cols], op=ALU.add)
             nc.sync.dma_start(out=out[P * j : P * (j + 1), cols], in_=result[:])
 
-        halves = []
-        early = range(EARLY)
-        second = range(EARLY, 2 * EARLY)
-
-        def encode_all(g, form):
-            for q in range(QUARTERS):
-                form(g, q)
-
-        def weigh_all(g, form):
-            for q in range(QUARTERS):
-                form(g, q)
-
-        def merge_all(g):
-            for half in range(2):
-                merge(g, half)
-
-        def moves(tiles, g):
-            for j in tiles:
-                move_pass(j, g, g == 0, False)
+        tile_piece = [(j, 0, F) for j in range(TILES)]
+        runs = [range(RUN * n, RUN * (n + 1)) for n in range(TILES // RUN)]
+        lower, upper = 0, RUN
+        all_quarters, all_groups, all_passes = range(QUARTERS), range(GROUPS), range(CAMERA_PASSES)
 
         deal_codes(0)
         deal_scales(0)
         deal_scales(1)
         deal_codes(1)
-        encode_all(0, encode_narrow)
-        encode_all(1, encode_narrow)
-        for j in early:
-            sort_camera(j)
-        weigh_all(0, weigh_narrow)
-        for j in early:
-            turn_camera(j)
-            gather_camera(j)
-        bias_rows = spread_bias()
+        encode(0, lower)
+        encode(1, upper)
+        sort_camera(runs[0])
+        weigh(0, all_quarters[:1])
         deal_scales(2)
+        weigh(0, all_quarters[1:])
+        turn_camera(runs[0], lower)
+        bias_rows = spread_bias(lower)
+
         deal_codes(2)
-        weigh_all(1, weigh_narrow)
-        encode_all(2, encode_narrow)
+        weigh(1, all_quarters)
+        encode(2, upper)
         quantise_h(0)
-        moves(early, 0)
+        for j in runs[0]:
+            open_piece(tile_piece[j], lower + j)
+            move_passes(tile_piece[j], [0])
         deal_scales(3)
         quantise_h(1)
-        moves(early, 1)
+        for j in runs[0]:
+            move_passes(tile_piece[j], [1])
+
         deal_codes(3)
         interleave_w(0, nc.scalar.copy)
-        weigh_all(2, weigh_narrow)
-        encode_all(3, encode_narrow)
-        for j in second:
-            sort_camera(j)
-        interleave_w(1, nc.scalar.copy)
+        weigh(2, all_quarters)
+        encode(3, upper)
+        sort_camera(runs[1])
         quantise_h(2)
-        moves(early, 2)
-        weigh_all(3, weigh_narrow)
-        ring.extend([0] * EARLY)
-        for j in second:
-            turn_camera(j)
-            gather_camera(j)
+        for j in runs[0]:
+            move_passes(tile_piece[j], [2])
+
+        weigh(3, all_quarters)
+        turn_camera(runs[1], upper)
         quantise_camera(0)
         quantise_h(3)
-        moves(early, 3)
-        quantise_camera(1)
-        quantise_camera(2)
-        quantise_camera(3)
+        for j in range(RUN, OPENED):
+            open_piece(tile_piece[j], j)
+            move_passes(tile_piece[j], all_groups[:-1])
+        for j in range(OPENED):
+            move_passes(tile_piece[j], all_groups[-1:])
+
         quantise_w(0)
-        ring.extend([0] * EARLY)
-        for g in range(MP):
-            moves([EARLY], g)
-        for j in early:
-            camera_pass(j, 0, False)
-        quantise_camera(EARLY)
-        quantise_w(1)
-        for j in early:
-            camera_pass(j, 1, True)
-        for k in range(DP):
-            camera_pass(EARLY, k, k == DP - 1)
-        for j in range(2 * EARLY, 3 * EARLY):
-            sort_camera(j)
-        done = []
-        for j in range(EARLY + 1, TILES):
+        for j in range(1, OPENED):
             quantise_camera(j)
-            for i in range(len(done), j - 1):
-                finish(i)
-                done.append(i)
-            if j == TILES - 1:
-                last_tile(j)
-            else:
-                for g in range(MP):
-                    move_pass(j, g, g == 0, False)
-                for k in range(DP):
-                    camera_pass(j, k, k == DP - 1)
-            if j % EARLY == 2 and j + 2 < TILES:
-                for i in range(j + 2, j + 2 + EARLY):
-                    turn_camera(i)
-                    gather_camera(i)
-                for i in range(j + 2 + EARLY, min(j + 2 + 2 * EARLY, TILES)):
-                    sort_camera(i)
-        finish(TILES - 2)
-        for part, cols in halves:
-            finish_half(TILES - 1, part, cols)
+        for j in range(OPENED):
+            camera_passes(tile_piece[j], all_passes[:1])
+        open_piece(tile_piece[OPENED], OPENED)
+        move_passes(tile_piece[OPENED], all_groups)
+        interleave_w(1, nc.vector.tensor_copy)
+        quantise_camera(OPENED)
+        quantise_w(1)
+        for j in range(OPENED):
+            camera_passes(tile_piece[j], all_passes[1:])
+        sort_camera(runs[2])
+        for j in range(OPENED - 1):
+            finish(tile_piece[j])
+        camera_passes(tile_piece[OPENED], all_passes)
+
+        free_bank = OPENED + 1
+        for j in range(OPENED + 1, TILES - 1):
+            if (j + 1) % RUN == 0:
+                coming = (j + 1) // RUN
+                turn_camera(runs[coming], free_bank)
+                free_bank = (free_bank + RUN) % BANKS
+                if coming + 1 < len(runs):
+                    sort_camera(runs[coming + 1])
+            quantise_camera(j)
+            finish(tile_piece[j - 2])
+            open_piece(tile_piece[j], free_bank)
+            free_bank = (free_bank + 1) % BANKS
+            move_passes(tile_piece[j], all_groups)
+            camera_passes(tile_piece[j], all_passes)
+
+        last = TILES - 1
+        halves = [(last, 0, F // 2), (last, F // 2, F)]
+        quantise_camera(last)
+        finish(tile_piece[last - 2])
+        for n, piece in enumerate(halves):
+            open_piece(piece, (free_bank + n) % BANKS)
+            move_passes(piece, all_groups)
+            camera_passes(piece, all_passes)
+        finish(tile_piece[last - 1])
+        for piece in halves:
+            finish(piece)

from contextlib import ExitStack

import concourse.mybir as mybir
from concourse.masks import make_identity

M, K, F, T, D = 2048, 1024, 512, 2048, 1024
FLOPS = 2 * (K * M * F + M * T * F + T * D * F)

F32 = mybir.dt.float32
BF16 = mybir.dt.bfloat16
I32 = mybir.dt.int32
U32 = mybir.dt.uint32
U16 = mybir.dt.uint16
U8 = mybir.dt.uint8
FP8X4 = mybir.dt.float8_e4m3fn_x4
FP4X4 = mybir.dt.float4_e2m1fn_x4
ALU = mybir.AluOpType

P = 128
PACK = 4
PASS = P * PACK
RADAR_PASSES = K // PASS
GROUPS = M // PASS
CAMERA_PASSES = D // PASS
TILES = T // P
QUARTERS = F // P
QUADRANTS = 4
CHUNK = 512
PAIR = 2
LINE = 16
BANKS = 8
RUN = BANKS // 2
OPENED = RUN + 2
DEPTH = 2 * RUN


def tile_radar_camera_fusion_s4_kernel(
    tc, radar_words, radar_scales, enc_words, enc_scales, trust, align_words, align_scales, camera, w_cam, bias, out
):
    nc = tc.nc
    with ExitStack() as ctx:
        keep = ctx.enter_context(tc.tile_pool(name="keep", bufs=1))
        stream = ctx.enter_context(tc.tile_pool(name="stream", bufs=RUN))
        psum = ctx.enter_context(tc.psum_pool(name="psum", bufs=1))
        ctx.enter_context(tc.manual_schedule())

        def kept(name, shape, dtype):
            return keep.tile(shape, dtype, name=name, align_bytes=64)

        def streamed(name, shape, dtype, bufs):
            return stream.tile(shape, dtype, name=name, bufs=bufs, align_bytes=64)

        def bank(index):
            return psum.tile([P, F], F32, name="bank%d" % index)

        r_raw = [kept("r_raw%d" % g, [P, RADAR_PASSES, 2 * PASS], U8) for g in range(GROUPS)]
        rs_raw = [kept("rs_raw%d" % h, [P, RADAR_PASSES, PAIR * PASS], U8) for h in range(GROUPS // PAIR)]
        e_codes = kept("e_codes", [P, RADAR_PASSES, 2 * F], U8)
        e_scales = kept("e_scales", [P, RADAR_PASSES, F], U8)
        a_codes = [kept("a_codes%d" % c, [P, GROUPS, CHUNK], U32) for c in range(T // CHUNK)]
        a_scales = kept("a_scales", [P, T], U8)
        cam_raw = [kept("cam_raw%d" % c, [P, PAIR, D], BF16) for c in range(TILES // PAIR)]
        w_raw = [kept("w_raw%d" % k, [P, PACK, F], BF16) for k in range(CAMERA_PASSES)]
        trust_sb = kept("trust_sb", [P, GROUPS, PACK], BF16)
        bias_col = kept("bias_col", [P, PACK], BF16)
        ident = kept("ident", [P, P], F32)

        nc.vector.memset(rs_raw[0][:].rearrange("p k n -> p (k n)").bitcast(I32), 0)
        nc.vector.memset(e_scales[:].rearrange("p k n -> p (k n)").bitcast(I32), 0)
        nc.vector.memset(rs_raw[1][:].rearrange("p k n -> p (k n)").bitcast(I32), 0)
        nc.vector.memset(a_scales[:].bitcast(I32), 0)
        make_identity(nc, ident[:])

        def load_radar(g):
            src = radar_words[:, :, 2 * PASS * g : 2 * PASS * (g + 1)].rearrange("k p n -> p k n")
            nc.sync.dma_start(out=r_raw[g][:].bitcast(I32), in_=src.bitcast(I32))

        def load_scale_rows(plane, rows):
            for q in range(QUADRANTS):
                src = rows[:, 4 * q : 4 * q + 4, :].rearrange("k r n -> r k n")
                nc.sync.dma_start(out=plane[32 * q : 32 * q + 4, :, :].bitcast(I32), in_=src.bitcast(I32))

        def load_radar_scales(h):
            load_scale_rows(rs_raw[h], radar_scales[:, :, PAIR * PASS * h : PAIR * PASS * (h + 1)])

        def load_align_scales():
            for q in range(QUADRANTS):
                src = align_scales[:, 4 * q : 4 * q + 4, :]
                nc.sync.dma_start(out=a_scales[32 * q : 32 * q + 16, :].bitcast(I32), in_=src.bitcast(I32))

        def load_align(c):
            src = align_words[:, :, CHUNK * c : CHUNK * (c + 1), :].rearrange("g p n t -> p g (n t)")
            nc.sync.dma_start(out=a_codes[c][:].bitcast(I32), in_=src.bitcast(I32))

        def load_camera(c):
            src = camera[PAIR * P * c : PAIR * P * (c + 1), :].rearrange("(j p) d -> p j d", p=P)
            nc.sync.dma_start(out=cam_raw[c][:], in_=src)

        def load_w(k):
            src = w_cam[PASS * k : PASS * (k + 1), :].rearrange("(p t) f -> p t f", t=PACK)
            nc.sync.dma_start(out=w_raw[k][:], in_=src)

        load_radar(0)
        load_radar_scales(0)
        nc.sync.dma_start(out=e_codes[:].bitcast(I32), in_=enc_words.rearrange("k p n -> p k n").bitcast(I32))
        load_scale_rows(e_scales, enc_scales)
        load_radar(1)
        nc.sync.dma_start(out=trust_sb[:], in_=trust.rearrange("(g p t) -> p g t", p=P, t=PACK))
        load_radar_scales(1)
        load_camera(0)
        load_camera(1)
        load_radar(2)
        nc.sync.dma_start(out=bias_col[:], in_=bias.rearrange("(p t) -> p t", t=PACK))
        load_align_scales()
        load_radar(3)
        load_align(0)
        load_w(0)
        load_camera(2)
        load_camera(3)
        load_align(1)
        load_w(1)
        for c in range(2, T // CHUNK):
            load_camera(2 * c)
            load_camera(2 * c + 1)
            load_align(c)

        r_codes, r_scales = {}, {}
        h_bank, h_rows, h_codes, h_scales = {}, {}, {}, {}
        w_rows, w_codes, w_scales = {}, {}, {}
        cam_sorted, cam_rows, cam_codes, cam_scales = {}, {}, {}, {}
        acc = {}

        def deal_codes(g):
            r_codes[g] = kept("r_codes%d" % g, [P, PACK, RADAR_PASSES, P], U16)
            nc.vector.tensor_copy(
                out=r_codes[g][:].rearrange("p t k (b i) -> p k b t i", i=LINE // 2),
                in_=r_raw[g][:].bitcast(U16).rearrange("p k (b i t) -> p k b t i", i=LINE // 2, t=PACK),
            )

        def deal_scales(g):
            r_scales[g] = kept("r_scales%d" % g, [P, PACK, RADAR_PASSES, P], U8)
            raw = rs_raw[g // PAIR][:, :, PASS * (g % PAIR) : PASS * (g % PAIR + 1)]
            nc.vector.tensor_copy(
                out=r_scales[g][:].rearrange("p t k (b i) -> p k b t i", i=LINE),
                in_=raw.rearrange("p k (b i t) -> p k b t i", i=LINE, t=PACK),
            )

        def encode(g, first_bank):
            for q in range(QUARTERS):
                h_bank[g, q] = bank(first_bank + q)
                for t in range(PACK):
                    for k in range(RADAR_PASSES):
                        nc.tensor.matmul_mx(
                            out=h_bank[g, q][:, P * t : P * (t + 1)],
                            lhsT=r_codes[g][:, t, k, :].bitcast(FP4X4),
                            lhsT_scale=r_scales[g][:, t, k, :],
                            rhs=e_codes[:, k, 2 * P * q : 2 * P * (q + 1)].bitcast(FP4X4),
                            rhs_scale=e_scales[:, k, P * q : P * (q + 1)],
                            start=(k == 0),
                            stop=(k == RADAR_PASSES - 1),
                        )

        def weigh(g, quarters):
            for q in quarters:
                if q == 0:
                    h_rows[g] = streamed("h_rows", [P, F, PACK], BF16, 2)
                nc.vector.scalar_tensor_tensor(
                    out=h_rows[g][:, P * q : P * (q + 1), :],
                    in0=h_bank[g, q][:].rearrange("p (t f) -> p f t", t=PACK),
                    scalar=0.0,
                    in1=trust_sb[:, g, :].unsqueeze(1).to_broadcast([P, P, PACK]),
                    op0=ALU.max,
                    op1=ALU.mult,
                )

        def quantise(rows, name, width):
            codes = kept(name + "_codes", [P, width], U32)
            scales = kept(name + "_scales", [P, width], U8)
            nc.vector.quantize_mx(out=codes[:].bitcast(FP8X4), scales=scales[:], in_=rows)
            return codes, scales

        def quantise_h(g):
            h_codes[g], h_scales[g] = quantise(h_rows[g][:].rearrange("p f t -> p (f t)"), "h%d" % g, F)

        def interleave_w(k, copy):
            w_rows[k] = kept("w_rows%d" % k, [P, F, PACK], BF16)
            copy(
                out=w_rows[k][:].rearrange("p (c i) t -> p c t i", i=4),
                in_=w_raw[k][:].rearrange("p t (c i) -> p c t i", i=4),
            )

        def quantise_w(k):
            w_codes[k], w_scales[k] = quantise(w_rows[k][:].rearrange("p f t -> p (f t)"), "w%d" % k, F)

        def sort_camera(tiles):
            for j in tiles:
                cam_sorted[j] = streamed("cam_sorted", [P, CAMERA_PASSES, 2, P], F32, RUN)
                pairs = cam_raw[j // PAIR][:, j % PAIR, :].bitcast(F32)
                nc.scalar.copy(
                    out=cam_sorted[j][:], in_=pairs.rearrange("p (k m u) -> p k u m", k=CAMERA_PASSES, u=2)
                )

        def turn_camera(tiles, first_bank):
            for n, j in enumerate(tiles):
                turned = bank((first_bank + n) % BANKS)
                for k in range(CAMERA_PASSES):
                    for u in range(2):
                        cols = slice(P * (2 * k + u), P * (2 * k + u + 1))
                        nc.tensor.transpose(turned[:, cols], cam_sorted[j][:, k, u, :], ident[:])
                cam_rows[j] = streamed("cam_rows", [P, CAMERA_PASSES, P, 2], F32, DEPTH)
                nc.scalar.copy(
                    out=cam_rows[j][:], in_=turned[:].rearrange("p (k u r) -> p k r u", k=CAMERA_PASSES, u=2)
                )

        def quantise_camera(j):
            rows = cam_rows[j][:].rearrange("p k r u -> p (k r u)").bitcast(BF16)
            cam_codes[j], cam_scales[j] = quantise(rows, "cam%d" % j, CAMERA_PASSES * P)

        def spread_bias(index):
            spread = bank(index)
            pairs = bias_col[:].bitcast(F32)
            for u in range(2):
                nc.tensor.transpose(spread[:, P * u : P * (u + 1)], pairs[:, u : u + 1].to_broadcast([P, P]), ident[:])
            rows = kept("bias_rows", [P, F], BF16)
            nc.scalar.copy(
                out=rows[:].bitcast(F32).rearrange("p (m u) -> p m u", u=2),
                in_=spread[:, : 2 * P].rearrange("p (u m) -> p m u", u=2),
            )
            return rows

        def open_piece(piece, index):
            whole_bank = bank(index)
            acc[piece] = whole_bank[:, : piece[2] - piece[1]]

        def move_passes(piece, groups):
            j, cols = piece[0], slice(piece[1], piece[2])
            col = P * j % CHUNK
            for g in groups:
                nc.tensor.matmul_mx(
                    out=acc[piece],
                    lhsT=a_codes[P * j // CHUNK][:, g, col : col + P].bitcast(FP8X4),
                    lhsT_scale=a_scales[4 * g :, P * j : P * (j + 1)],
                    rhs=h_codes[g][:, cols].bitcast(FP8X4),
                    rhs_scale=h_scales[g][:, cols],
                    start=(g == 0),
                    stop=False,
                )

        def camera_passes(piece, passes):
            j, cols = piece[0], slice(piece[1], piece[2])
            for k in passes:
                nc.tensor.matmul_mx(
                    out=acc[piece],
                    lhsT=cam_codes[j][:, P * k : P * (k + 1)].bitcast(FP8X4),
                    lhsT_scale=cam_scales[j][:, P * k : P * (k + 1)],
                    rhs=w_codes[k][:, cols].bitcast(FP8X4),
                    rhs_scale=w_scales[k][:, cols],
                    start=False,
                    stop=(k == CAMERA_PASSES - 1),
                )

        def finish(piece):
            j, cols = piece[0], slice(piece[1], piece[2])
            result = streamed("result", [P, piece[2] - piece[1]], F32, DEPTH)
            nc.vector.tensor_tensor(out=result[:], in0=acc[piece], in1=bias_rows[:, cols], op=ALU.add)
            nc.sync.dma_start(out=out[P * j : P * (j + 1), cols], in_=result[:])

        tile_piece = [(j, 0, F) for j in range(TILES)]
        runs = [range(RUN * n, RUN * (n + 1)) for n in range(TILES // RUN)]
        lower, upper = 0, RUN
        all_quarters, all_groups, all_passes = range(QUARTERS), range(GROUPS), range(CAMERA_PASSES)

        deal_codes(0)
        deal_scales(0)
        deal_scales(1)
        deal_codes(1)
        encode(0, lower)
        encode(1, upper)
        sort_camera(runs[0])
        weigh(0, all_quarters[:1])
        deal_scales(2)
        weigh(0, all_quarters[1:])
        turn_camera(runs[0], lower)
        bias_rows = spread_bias(lower)

        deal_codes(2)
        weigh(1, all_quarters)
        encode(2, upper)
        quantise_h(0)
        for j in runs[0]:
            open_piece(tile_piece[j], lower + j)
            move_passes(tile_piece[j], [0])
        deal_scales(3)
        quantise_h(1)
        for j in runs[0]:
            move_passes(tile_piece[j], [1])

        deal_codes(3)
        interleave_w(0, nc.scalar.copy)
        weigh(2, all_quarters)
        encode(3, upper)
        sort_camera(runs[1])
        quantise_h(2)
        for j in runs[0]:
            move_passes(tile_piece[j], [2])

        weigh(3, all_quarters)
        turn_camera(runs[1], upper)
        quantise_camera(0)
        quantise_h(3)
        for j in range(RUN, OPENED):
            open_piece(tile_piece[j], j)
            move_passes(tile_piece[j], all_groups[:-1])
        for j in range(OPENED):
            move_passes(tile_piece[j], all_groups[-1:])

        quantise_w(0)
        for j in range(1, OPENED):
            quantise_camera(j)
        for j in range(OPENED):
            camera_passes(tile_piece[j], all_passes[:1])
        open_piece(tile_piece[OPENED], OPENED)
        move_passes(tile_piece[OPENED], all_groups)
        interleave_w(1, nc.vector.tensor_copy)
        quantise_camera(OPENED)
        quantise_w(1)
        for j in range(OPENED):
            camera_passes(tile_piece[j], all_passes[1:])
        sort_camera(runs[2])
        for j in range(OPENED - 1):
            finish(tile_piece[j])
        camera_passes(tile_piece[OPENED], all_passes)

        free_bank = OPENED + 1
        for j in range(OPENED + 1, TILES - 1):
            if (j + 1) % RUN == 0:
                coming = (j + 1) // RUN
                turn_camera(runs[coming], free_bank)
                free_bank = (free_bank + RUN) % BANKS
                if coming + 1 < len(runs):
                    sort_camera(runs[coming + 1])
            quantise_camera(j)
            finish(tile_piece[j - 2])
            open_piece(tile_piece[j], free_bank)
            free_bank = (free_bank + 1) % BANKS
            move_passes(tile_piece[j], all_groups)
            camera_passes(tile_piece[j], all_passes)

        last = TILES - 1
        halves = [(last, 0, F // 2), (last, F // 2, F)]
        quantise_camera(last)
        finish(tile_piece[last - 2])
        for n, piece in enumerate(halves):
            open_piece(piece, (free_bank + n) % BANKS)
            move_passes(piece, all_groups)
            camera_passes(piece, all_passes)
        finish(tile_piece[last - 1])
        for piece in halves:
            finish(piece)
